import numpy as np
import ml_dtypes


def mxq(x, axis, fmt="e4m3"):
    dtype, down = {"e4m3": (ml_dtypes.float8_e4m3fn, 7), "e5m2": (ml_dtypes.float8_e5m2, 14)}[fmt]
    v = np.moveaxis(np.asarray(x, np.float32).astype(ml_dtypes.bfloat16).astype(np.float64), axis, -1)
    blocks = v.reshape(v.shape[:-1] + (-1, 32))
    amax = np.abs(blocks).max(-1, keepdims=True)
    byte = np.maximum(np.where(amax > 0, np.frexp(amax)[1] - 1 + 127, 0) - down, 1)
    scale = np.exp2(byte - 127.0)
    codes = (blocks / scale).astype(np.float32).astype(dtype).astype(np.float64)
    return np.moveaxis((codes * scale).reshape(v.shape), -1, axis)


WIDE = False


def mx_kscale(k):
    if not WIDE:
        return np.ones(k)
    levels = np.array([24, -24, 12, -12, 0])
    if k % 512:
        return np.exp2(np.random.permutation(np.resize(levels, k // 32))).repeat(32)
    a = np.empty((k // 512, 16))
    for p in range(k // 512):
        a[p, :8] = np.random.permutation(np.resize(levels, 8))
        for g in range(8):
            far = levels[np.abs(levels - a[p, g]) >= 10]
            a[p, g + 8] = far[np.random.randint(len(far))]
    return np.exp2(a.ravel()).repeat(32)


def f64(x):
    return np.asarray(x).astype(np.float64)


def striped8(idx):
    return np.concatenate([v.reshape(-1, 16).T for v in idx]).astype(np.uint16)


def unstriped8(offs):
    return np.stack([offs[16 * g:16 * g + 16].T.reshape(-1) for g in range(8)]).astype(np.int64)


E2M1 = np.array([0.0, 0.5, 1.0, 1.5, 2.0, 3.0, 4.0, 6.0, -0.0, -0.5, -1.0, -1.5, -2.0, -3.0, -4.0, -6.0])


def pack_weight(w, fmt):
    k, n = w.shape
    w = f64(np.asarray(w, np.float32).astype(ml_dtypes.bfloat16)).reshape(k // 32, 32, n)
    amax = np.abs(w).max(1)
    if fmt == "e4m3":
        byte = np.frexp(amax)[1] - 1 + 127 - 7
    else:
        mant, ex = np.frexp(amax / 6.0)
        byte = np.where(mant > 0.5, ex, ex - 1) + 127
    byte = np.clip(np.where(amax > 0, byte, 1), 1, 254)
    scaled = (w * np.exp2(127.0 - byte)[:, None, :]).reshape(k, n).astype(np.float32)
    by_word = np.ascontiguousarray(scaled.reshape(k // 512, 128, 4, n).transpose(0, 1, 3, 2))
    if fmt == "e4m3":
        words = by_word.astype(ml_dtypes.float8_e4m3fn).view(np.uint8)
    else:
        c = by_word.astype(ml_dtypes.float4_e2m1fn).view(np.uint8) & 0xF
        words = (c[..., 0::2] | (c[..., 1::2] << 4)).reshape(k // 512, 128, 2 * n)
    return np.ascontiguousarray(words), np.ascontiguousarray(byte.astype(np.uint8).reshape(k // 512, 16, n))


def unpack_weight(words, scales, fmt):
    g, _, n = scales.shape
    words = np.ascontiguousarray(words).reshape(g, 128, n, -1)
    if fmt == "e4m3":
        vals = words.view(ml_dtypes.float8_e4m3fn).astype(np.float64)
    else:
        nib = np.empty((g, 128, n, 4), np.uint8)
        nib[..., 0::2] = words & 0xF
        nib[..., 1::2] = words >> 4
        vals = E2M1[nib]
    vals = vals * np.repeat(np.exp2(scales.astype(np.float64) - 127.0), 8, axis=1)[..., None]
    return vals.transpose(0, 1, 3, 2).reshape(g * 512, n)


def silu(f):
    return f / (1.0 + np.exp(-np.maximum(f, -700.0)))


def sigm(f):
    return 1.0 / (1.0 + np.exp(-np.maximum(f, -700.0)))


K, L, N, T, J = 512, 512, 512, 2048, 1024


def setup_inputs():
    n = np.random.standard_normal
    s = mx_kscale(K)[:, None]
    s2 = mx_kscale(L)[:, None]
    p_wb = pack_weight(n((L, N)) / np.sqrt(L) / s2, "e2m1")
    return {
        "xT": (n((K, T)) * s).astype(np.float32),
        "wgt": np.repeat(np.random.uniform(0.5, 2.0, (8, J)), 16, axis=0).astype(np.float32),
        "zT": (n((L, T)) * s2).astype(np.float32),
        "wgt2": np.repeat(np.random.uniform(0.5, 2.0, (8, J)), 16, axis=0).astype(np.float32),
        "wa": (n((K, N)) / np.sqrt(K) / s).astype(np.float32),
        "wb_words": p_wb[0],
        "wb_scales": p_wb[1],
        "b": (0.3 * n(N)).astype(np.float32),
        "offs": striped8(np.stack([np.random.permutation(T)[:J] for _ in range(8)])),
        "offs2": striped8(np.stack([np.random.permutation(T)[:J] for _ in range(8)])),
    }


def reference(xT, wgt, zT, wgt2, wa, wb_words, wb_scales, b, offs, offs2):
    idx = unstriped8(offs)
    idx2 = unstriped8(offs2)
    rows = np.arange(K)
    xg = f64(wgt)[rows // 4 % 128] * f64(xT)[rows[:, None], idx[rows % 512 // 64]]
    xT_ = mxq(xg, 0, "e4m3")
    rows = np.arange(L)
    xg = f64(wgt2)[rows // 4 % 128] * f64(zT)[rows[:, None], idx2[rows % 512 // 64]]
    zT_ = mxq(xg, 0, "e4m3")
    wa_ = mxq(f64(wa), 0, "e4m3")
    wb_ = unpack_weight(wb_words, wb_scales, "e2m1")
    ya = wa_.T @ xT_
    yb = wb_.T @ zT_
    return silu(ya * sigm(yb) + f64(b)[:, None])

@@ -1,0 +1,184 @@
+from contextlib import ExitStack
+
+import concourse.mybir as mybir
+
+K, L, N, T, J = 512, 512, 512, 2048, 1024
+FLOPS = 2 * (K + L) * N * J
+
+F32 = mybir.dt.float32
+BF16 = mybir.dt.bfloat16
+I32 = mybir.dt.int32
+U32 = mybir.dt.uint32
+U16 = mybir.dt.uint16
+U8 = mybir.dt.uint8
+FP8X4 = mybir.dt.float8_e4m3fn_x4
+FP4X4 = mybir.dt.float4_e2m1fn_x4
+ALU = mybir.AluOpType
+ACT = mybir.ActivationFunctionType
+
+P = 128
+PACK = 4
+GROUP = 16
+BANK = 512
+N_TILES = N // P
+Z_WIDTHS = (512, 512)
+X_WIDTHS = (256, 256, 256, 128, 128)
+
+
+def spans(widths):
+    return [(sum(widths[:s]), w) for s, w in enumerate(widths)]
+
+
+def interleave(copy, dst, src):
+    copy(
+        out=dst.rearrange("p (c e) i -> p c i e", e=4),
+        in_=src.rearrange("p i (c e) -> p c i e", e=4),
+    )
+
+
+def quantize(nc, codes, scales, grouped):
+    nc.vector.quantize_mx(
+        out=codes[:].bitcast(FP8X4),
+        scales=scales[:],
+        in_=grouped[:].rearrange("p w i -> p (w i)"),
+    )
+
+
+def tile_list_gate_silu_kernel(
+    tc, xT, wgt, zT, wgt2, wa, wb_words, wb_scales, b, offs, offs2, out
+):
+    nc = tc.nc
+    with ExitStack() as ctx:
+        sb = ctx.enter_context(tc.tile_pool(name="sb", bufs=1))
+        ps = ctx.enter_context(tc.psum_pool(name="ps", bufs=1))
+
+        z_spans, x_spans = spans(Z_WIDTHS), spans(X_WIDTHS)
+        z_list = sb.tile([P, J // GROUP], U16, name="z_list")
+        x_list = sb.tile([P, J // GROUP], U16, name="x_list")
+        z_planes = [sb.tile([P, T], F32, name=f"z_plane{i}") for i in range(PACK)]
+        x_planes = [sb.tile([P, T], F32, name=f"x_plane{i}") for i in range(PACK)]
+        z_wgt = sb.tile([P, J], F32, name="z_wgt")
+        x_wgt = sb.tile([P, J], F32, name="x_wgt")
+        wa_raw = sb.tile([P, PACK, N], F32, name="wa_raw")
+        wb_codes = sb.tile([P, 2 * N], U8, name="wb_codes", align_bytes=64)
+        wb_plane = sb.tile([P, N], U8, name="wb_plane", align_bytes=64)
+        bias = sb.tile([P, N_TILES], F32, name="bias")
+
+        z_rows = zT.rearrange("(p i) t -> i p t", i=PACK)
+        x_rows = xT.rearrange("(p i) t -> i p t", i=PACK)
+
+        nc.vector.memset(wb_plane[:].bitcast(I32), 0)
+        warm = sb.tile([P, 8], F32, name="warm")
+        warm2 = sb.tile([P, 8], F32, name="warm2")
+        nc.vector.memset(warm[:], 0.0)
+        nc.scalar.activation(out=warm2[:, 0:1], in_=warm[:, 0:1], func=ACT.Silu)
+        nc.sync.dma_start(z_list[:], offs2)
+        nc.sync.dma_start(z_planes[0][:], z_rows[0])
+        for s, (j0, w) in enumerate(z_spans):
+            nc.sync.dma_start(z_wgt[:, j0 : j0 + w], wgt2[:, j0 : j0 + w])
+        for i in range(1, PACK):
+            nc.sync.dma_start(z_planes[i][:], z_rows[i])
+        nc.sync.dma_start(x_list[:], offs)
+        nc.sync.dma_start(x_planes[0][:], x_rows[0])
+        nc.sync.dma_start(x_wgt[:], wgt)
+        nc.sync.dma_start(wb_codes[:].bitcast(I32), wb_words[0].bitcast(I32))
+        for q in range(4):
+            nc.sync.dma_start(
+                wb_plane[32 * q : 32 * q + 4, :].bitcast(I32),
+                wb_scales[0, 4 * q : 4 * q + 4, :].bitcast(I32),
+            )
+        nc.sync.dma_start(x_planes[1][:], x_rows[1])
+        for i in range(2, PACK):
+            nc.sync.dma_start(x_planes[i][:], x_rows[i])
+        nc.sync.dma_start(wa_raw[:], wa.rearrange("(p i) n -> p i n", i=PACK))
+        with nc.allow_non_contiguous_dma(reason="one bias value a partition"):
+            nc.sync.dma_start(bias[:], b.rearrange("(t p) -> p t", p=P))
+
+        def gather(dst, plane, lst, weights, j0, w):
+            nc.vector.tensor_tensor(
+                dst,
+                plane[:].indirect(lst[:, j0 // GROUP : (j0 + w) // GROUP]),
+                weights,
+                ALU.mult,
+            )
+
+        z_picked = sb.tile([P, PACK, J], F32, name="z_picked")
+        for i in range(PACK):
+            for j0, w in z_spans if i in (0, PACK - 1) else [(0, J)]:
+                gather(z_picked[:, i, j0 : j0 + w], z_planes[i], z_list, z_wgt[:, j0 : j0 + w], j0, w)
+
+        gate = sb.tile([P, N_TILES, J], F32, name="gate")
+        for s, (j0, w) in enumerate(z_spans):
+            grouped = sb.tile([P, w, PACK], BF16, name=f"z_grouped{s}", align_bytes=64)
+            codes = sb.tile([P, w], U32, name=f"z_codes{s}", align_bytes=64)
+            scales = sb.tile([P, w], U8, name=f"z_scales{s}", align_bytes=64)
+            interleave(nc.scalar.copy, grouped[:], z_picked[:, :, j0 : j0 + w])
+            quantize(nc, codes, scales, grouped)
+            for t in range(N_TILES):
+                acc = ps.tile([P, BANK], F32, name=f"yb{s}_{t}", tag=f"bank{(s * N_TILES + t) % 8}")
+                nc.tensor.matmul_mx(
+                    out=acc[:],
+                    lhsT=wb_codes[:, 2 * P * t : 2 * P * (t + 1)].bitcast(FP4X4),
+                    lhsT_scale=wb_plane[:, P * t : P * (t + 1)],
+                    rhs=codes[:].bitcast(FP8X4),
+                    rhs_scale=scales[:],
+                    start=True,
+                    stop=True,
+                )
+                nc.scalar.activation(out=gate[:, t, j0 : j0 + w], in_=acc[:], func=ACT.Tanh, scale=0.5)
+
+        x_picked = sb.tile([P, PACK, J], F32, name="x_picked")
+        for i in range(PACK):
+            for j0, w in x_spans if i == PACK - 1 else [(0, J)]:
+                gather(x_picked[:, i, j0 : j0 + w], x_planes[i], x_list, x_wgt[:, j0 : j0 + w], j0, w)
+
+        half = N // 2
+        wa_grouped = [sb.tile([P, half, PACK], BF16, name=f"wa_grouped{h}", align_bytes=64) for h in range(2)]
+        wa_codes = [sb.tile([P, half], U32, name=f"wa_codes{h}", align_bytes=64) for h in range(2)]
+        wa_plane = [sb.tile([P, half], U8, name=f"wa_plane{h}", align_bytes=64) for h in range(2)]
+        for h in range(2):
+            interleave(nc.vector.tensor_copy, wa_grouped[h][:], wa_raw[:, :, h * half : (h + 1) * half])
+        for h in range(2):
+            quantize(nc, wa_codes[h], wa_plane[h], wa_grouped[h])
+
+        out_tiles = out.rearrange("(t p) j -> p t j", p=P)
+        banks_used = 0
+        for s, (j0, w) in enumerate(x_spans):
+            grouped = sb.tile([P, w, PACK], BF16, name=f"x_grouped{s}", align_bytes=64)
+            codes = sb.tile([P, w], U32, name=f"x_codes{s}", align_bytes=64)
+            scales = sb.tile([P, w], U8, name=f"x_scales{s}", align_bytes=64)
+            gated = sb.tile([P, N_TILES, w], F32, name=f"gated{s}")
+            result = sb.tile([P, N_TILES, w], F32, name=f"result{s}")
+            interleave(nc.scalar.copy, grouped[:], x_picked[:, :, j0 : j0 + w])
+            quantize(nc, codes, scales, grouped)
+            per_bank = BANK // w
+            for t0 in range(0, N_TILES, per_bank):
+                acc = ps.tile([P, per_bank, w], F32, name=f"ya{s}_{t0}", tag=f"bank{banks_used % 8}")
+                banks_used = banks_used + 1
+                for t in range(t0, t0 + per_bank):
+                    nc.tensor.matmul_mx(
+                        out=acc[:, t - t0, :],
+                        lhsT=wa_codes[t // 2][:, P * (t % 2) : P * (t % 2 + 1)].bitcast(FP8X4),
+                        lhsT_scale=wa_plane[t // 2][:, P * (t % 2) : P * (t % 2 + 1)],
+                        rhs=codes[:].bitcast(FP8X4),
+                        rhs_scale=scales[:],
+                        start=True,
+                        stop=True,
+                    )
+                nc.vector.scalar_tensor_tensor(
+                    out=gated[:, t0 : t0 + per_bank, :],
+                    in0=gate[:, t0 : t0 + per_bank, j0 : j0 + w],
+                    scalar=1.0,
+                    in1=acc[:],
+                    op0=ALU.add,
+                    op1=ALU.mult,
+                )
+                for t in range(t0, t0 + per_bank):
+                    nc.scalar.activation(
+                        out=result[:, t, :],
+                        in_=gated[:, t, :],
+                        func=ACT.Silu,
+                        bias=bias[:, t : t + 1],
+                        scale=0.5,
+                    )
+            nc.sync.dma_start(out_tiles[:, :, j0 : j0 + w], result[:])

@@ -1,6 +1,7 @@
 from contextlib import ExitStack
 
 import concourse.mybir as mybir
+from concourse.masks import make_identity
 
 K, L, N, T, J = 512, 512, 512, 2048, 1024
 FLOPS = 2 * (K + L) * N * J
@@ -21,8 +22,8 @@ PACK = 4
 GROUP = 16
 BANK = 512
 N_TILES = N // P
-Z_WIDTHS = (512, 512)
-X_WIDTHS = (256, 256, 256, 128, 128)
+Z_WIDTHS = (256, 256, 512)
+X_WIDTHS = (256, 256, 256, 256)
 
 
 def spans(widths):
@@ -56,7 +57,7 @@ def tile_list_gate_silu_kernel(
         z_list = sb.tile([P, J // GROUP], U16, name="z_list")
         x_list = sb.tile([P, J // GROUP], U16, name="x_list")
         z_planes = [sb.tile([P, T], F32, name=f"z_plane{i}") for i in range(PACK)]
-        x_planes = [sb.tile([P, T], F32, name=f"x_plane{i}") for i in range(PACK)]
+        x_planes = [sb.tile([P, T], F32, name=f"x_plane{i}", tag=f"x_plane{i}", align_bytes=64) for i in range(PACK)]
         z_wgt = sb.tile([P, J], F32, name="z_wgt")
         x_wgt = sb.tile([P, J], F32, name="x_wgt")
         wa_raw = sb.tile([P, PACK, N], F32, name="wa_raw")
@@ -67,20 +68,29 @@ def tile_list_gate_silu_kernel(
         z_rows = zT.rearrange("(p i) t -> i p t", i=PACK)
         x_rows = xT.rearrange("(p i) t -> i p t", i=PACK)
 
-        nc.vector.memset(wb_plane[:].bitcast(I32), 0)
+        half_j = J // 2
+        rows = sb.tile([P, half_j], F32, name="rows")
+        ident = sb.tile([P, P], F32, name="ident")
         warm = sb.tile([P, 8], F32, name="warm")
         warm2 = sb.tile([P, 8], F32, name="warm2")
+        nc.vector.memset(rows[:], 0.0)
         nc.vector.memset(warm[:], 0.0)
+        nc.vector.memset(wb_plane[:].bitcast(I32), 0)
         nc.scalar.activation(out=warm2[:, 0:1], in_=warm[:, 0:1], func=ACT.Silu)
+        make_identity(nc, ident[:])
+
         nc.sync.dma_start(z_list[:], offs2)
         nc.sync.dma_start(z_planes[0][:], z_rows[0])
-        for s, (j0, w) in enumerate(z_spans):
-            nc.sync.dma_start(z_wgt[:, j0 : j0 + w], wgt2[:, j0 : j0 + w])
+        nc.sync.dma_start(z_wgt[:, :half_j], wgt2[:, :half_j])
+        nc.sync.dma_start(z_wgt[:, half_j:], wgt2[:, half_j:])
+        head_rows = wgt.rearrange("(g r) j -> r g j", r=GROUP)[0]
+        nc.sync.dma_start(rows[0:8, :], head_rows[:, :half_j])
+        nc.sync.dma_start(rows[8:16, :], head_rows[:, half_j:])
+        nc.sync.dma_start(rows[16:20, 0:P], b.rearrange("(t p) -> t p", p=P))
         for i in range(1, PACK):
             nc.sync.dma_start(z_planes[i][:], z_rows[i])
         nc.sync.dma_start(x_list[:], offs)
         nc.sync.dma_start(x_planes[0][:], x_rows[0])
-        nc.sync.dma_start(x_wgt[:], wgt)
         nc.sync.dma_start(wb_codes[:].bitcast(I32), wb_words[0].bitcast(I32))
         for q in range(4):
             nc.sync.dma_start(
@@ -88,11 +98,29 @@ def tile_list_gate_silu_kernel(
                 wb_scales[0, 4 * q : 4 * q + 4, :].bitcast(I32),
             )
         nc.sync.dma_start(x_planes[1][:], x_rows[1])
-        for i in range(2, PACK):
-            nc.sync.dma_start(x_planes[i][:], x_rows[i])
+        nc.sync.dma_start(x_planes[2][:], x_rows[2])
         nc.sync.dma_start(wa_raw[:], wa.rearrange("(p i) n -> p i n", i=PACK))
-        with nc.allow_non_contiguous_dma(reason="one bias value a partition"):
-            nc.sync.dma_start(bias[:], b.rearrange("(t p) -> p t", p=P))
+        nc.sync.dma_start(x_planes[3][:], x_rows[3])
+
+        def turn(src, name, bank):
+            turned = ps.tile([P, 4, P], F32, name=name, tag=f"bank{bank}")
+            for c in range(4):
+                nc.tensor.transpose(turned[:, c, :], src[:, c * P : (c + 1) * P], ident[:])
+            return turned
+
+        def spread(turned, row0, dst, name, bank):
+            wide = sb.tile([P, half_j], F32, name=name)
+            nc.scalar.copy(
+                out=wide[:].rearrange("p (c g r) -> p c g r", c=4, r=GROUP),
+                in_=turned[:, :, row0 : row0 + 8].unsqueeze(3).to_broadcast([P, 4, 8, GROUP]),
+            )
+            back = turn(wide[:], name + "_back", bank)
+            nc.scalar.copy(out=dst, in_=back[:].rearrange("p c j -> p (c j)"))
+
+        turned = turn(rows[:], "turned", 0)
+        spread(turned, 0, x_wgt[:, :half_j], "x_wide0", 1)
+        spread(turned, 8, x_wgt[:, half_j:], "x_wide1", 2)
+        nc.scalar.copy(out=bias[:], in_=turned[:, 0, 16:20])
 
         def gather(dst, plane, lst, weights, j0, w):
             nc.vector.tensor_tensor(
@@ -103,43 +131,62 @@ def tile_list_gate_silu_kernel(
             )
 
         z_picked = sb.tile([P, PACK, J], F32, name="z_picked")
+        z_grouped = [
+            sb.tile([P, w, PACK], BF16, name=f"z_grouped{s}", align_bytes=64) for s, (j0, w) in enumerate(z_spans)
+        ]
         for i in range(PACK):
-            for j0, w in z_spans if i in (0, PACK - 1) else [(0, J)]:
+            for j0, w in {0: spans((half_j, half_j)), PACK - 1: z_spans}.get(i, [(0, J)]):
                 gather(z_picked[:, i, j0 : j0 + w], z_planes[i], z_list, z_wgt[:, j0 : j0 + w], j0, w)
+            if i == 1:
+                for s, (j0, w) in enumerate(z_spans):
+                    interleave(nc.scalar.copy, z_grouped[s][:, :, 0:2], z_picked[:, 0:2, j0 : j0 + w])
 
         gate = sb.tile([P, N_TILES, J], F32, name="gate")
-        for s, (j0, w) in enumerate(z_spans):
-            grouped = sb.tile([P, w, PACK], BF16, name=f"z_grouped{s}", align_bytes=64)
-            codes = sb.tile([P, w], U32, name=f"z_codes{s}", align_bytes=64)
+
+        def gate_slice(s, codes_tag):
+            j0, w = z_spans[s]
+            grouped = z_grouped[s]
+            codes = sb.tile([P, w], U32, name=f"z_codes{s}", tag=codes_tag, align_bytes=64)
             scales = sb.tile([P, w], U8, name=f"z_scales{s}", align_bytes=64)
-            interleave(nc.scalar.copy, grouped[:], z_picked[:, :, j0 : j0 + w])
+            interleave(nc.scalar.copy, grouped[:, :, 2:4], z_picked[:, 2:4, j0 : j0 + w])
             quantize(nc, codes, scales, grouped)
-            for t in range(N_TILES):
-                acc = ps.tile([P, BANK], F32, name=f"yb{s}_{t}", tag=f"bank{(s * N_TILES + t) % 8}")
-                nc.tensor.matmul_mx(
-                    out=acc[:],
-                    lhsT=wb_codes[:, 2 * P * t : 2 * P * (t + 1)].bitcast(FP4X4),
-                    lhsT_scale=wb_plane[:, P * t : P * (t + 1)],
-                    rhs=codes[:].bitcast(FP8X4),
-                    rhs_scale=scales[:],
-                    start=True,
-                    stop=True,
+            per_bank = BANK // w
+            for t0 in range(0, N_TILES, per_bank):
+                bank = (j0 * N_TILES + t0 * w) // BANK
+                acc = ps.tile([P, per_bank, w], F32, name=f"yb{s}_{t0}", tag=f"bank{bank}")
+                for t in range(t0, t0 + per_bank):
+                    nc.tensor.matmul_mx(
+                        out=acc[:, t - t0, :],
+                        lhsT=wb_codes[:, 2 * P * t : 2 * P * (t + 1)].bitcast(FP4X4),
+                        lhsT_scale=wb_plane[:, P * t : P * (t + 1)],
+                        rhs=codes[:].bitcast(FP8X4),
+                        rhs_scale=scales[:],
+                        start=True,
+                        stop=True,
+                    )
+                nc.scalar.activation(
+                    out=gate[:, t0 : t0 + per_bank, j0 : j0 + w], in_=acc[:], func=ACT.Tanh, scale=0.5
                 )
-                nc.scalar.activation(out=gate[:, t, j0 : j0 + w], in_=acc[:], func=ACT.Tanh, scale=0.5)
 
         x_picked = sb.tile([P, PACK, J], F32, name="x_picked")
-        for i in range(PACK):
+
+        def gather_x(i):
             for j0, w in x_spans if i == PACK - 1 else [(0, J)]:
                 gather(x_picked[:, i, j0 : j0 + w], x_planes[i], x_list, x_wgt[:, j0 : j0 + w], j0, w)
 
-        half = N // 2
-        wa_grouped = [sb.tile([P, half, PACK], BF16, name=f"wa_grouped{h}", align_bytes=64) for h in range(2)]
-        wa_codes = [sb.tile([P, half], U32, name=f"wa_codes{h}", align_bytes=64) for h in range(2)]
-        wa_plane = [sb.tile([P, half], U8, name=f"wa_plane{h}", align_bytes=64) for h in range(2)]
-        for h in range(2):
-            interleave(nc.vector.tensor_copy, wa_grouped[h][:], wa_raw[:, :, h * half : (h + 1) * half])
-        for h in range(2):
-            quantize(nc, wa_codes[h], wa_plane[h], wa_grouped[h])
+        last_z = len(z_spans) - 1
+        for s in range(last_z):
+            gate_slice(s, f"z_codes{s}")
+        gather_x(0)
+        gate_slice(last_z, "x_plane0")
+        for i in range(1, PACK):
+            gather_x(i)
+
+        wa_grouped = sb.tile([P, N, PACK], BF16, name="wa_grouped", align_bytes=64)
+        wa_codes = sb.tile([P, N], U32, name="wa_codes", tag=f"x_plane{PACK - 1}", align_bytes=64)
+        wa_plane = sb.tile([P, N], U8, name="wa_plane", align_bytes=64)
+        interleave(nc.scalar.copy, wa_grouped[:], wa_raw[:])
+        quantize(nc, wa_codes, wa_plane, wa_grouped)
 
         out_tiles = out.rearrange("(t p) j -> p t j", p=P)
         banks_used = 0
@@ -149,7 +196,7 @@ def tile_list_gate_silu_kernel(
             scales = sb.tile([P, w], U8, name=f"x_scales{s}", align_bytes=64)
             gated = sb.tile([P, N_TILES, w], F32, name=f"gated{s}")
             result = sb.tile([P, N_TILES, w], F32, name=f"result{s}")
-            interleave(nc.scalar.copy, grouped[:], x_picked[:, :, j0 : j0 + w])
+            interleave(nc.vector.tensor_copy if s == len(x_spans) - 1 else nc.scalar.copy, grouped[:], x_picked[:, :, j0 : j0 + w])
             quantize(nc, codes, scales, grouped)
             per_bank = BANK // w
             for t0 in range(0, N_TILES, per_bank):
@@ -158,8 +205,8 @@ def tile_list_gate_silu_kernel(
                 for t in range(t0, t0 + per_bank):
                     nc.tensor.matmul_mx(
                         out=acc[:, t - t0, :],
-                        lhsT=wa_codes[t // 2][:, P * (t % 2) : P * (t % 2 + 1)].bitcast(FP8X4),
-                        lhsT_scale=wa_plane[t // 2][:, P * (t % 2) : P * (t % 2 + 1)],
+                        lhsT=wa_codes[:, P * t : P * (t + 1)].bitcast(FP8X4),
+                        lhsT_scale=wa_plane[:, P * t : P * (t + 1)],
                         rhs=codes[:].bitcast(FP8X4),
                         rhs_scale=scales[:],
                         start=True,
@@ -181,4 +228,4 @@ def tile_list_gate_silu_kernel(
                         bias=bias[:, t : t + 1],
                         scale=0.5,
                     )
-            nc.sync.dma_start(out_tiles[:, :, j0 : j0 + w], result[:])
+                nc.sync.dma_start(out_tiles[:, t0 : t0 + per_bank, j0 : j0 + w], result[:, t0 : t0 + per_bank, :])

@@ -60,7 +60,7 @@ def tile_list_gate_silu_kernel(
         x_planes = [sb.tile([P, T], F32, name=f"x_plane{i}", tag=f"x_plane{i}", align_bytes=64) for i in range(PACK)]
         z_wgt = sb.tile([P, J], F32, name="z_wgt")
         x_wgt = sb.tile([P, J], F32, name="x_wgt")
-        wa_raw = sb.tile([P, PACK, N], F32, name="wa_raw")
+        wa_raw = [sb.tile([P, PACK, N // 2], F32, name=f"wa_raw{h}") for h in range(2)]
         wb_codes = sb.tile([P, 2 * N], U8, name="wb_codes", align_bytes=64)
         wb_plane = sb.tile([P, N], U8, name="wb_plane", align_bytes=64)
         bias = sb.tile([P, N_TILES], F32, name="bias")
@@ -98,9 +98,13 @@ def tile_list_gate_silu_kernel(
                 wb_scales[0, 4 * q : 4 * q + 4, :].bitcast(I32),
             )
         nc.sync.dma_start(x_planes[1][:], x_rows[1])
-        nc.sync.dma_start(x_planes[2][:], x_rows[2])
-        nc.sync.dma_start(wa_raw[:], wa.rearrange("(p i) n -> p i n", i=PACK))
+        wa_rows = wa.rearrange("(p i) n -> p i n", i=PACK)
+        held = T - T // 8
+        nc.sync.dma_start(wa_raw[0][:], wa_rows[:, :, : N // 2])
+        nc.sync.dma_start(x_planes[2][:, :held], x_rows[2][:, :held])
         nc.sync.dma_start(x_planes[3][:], x_rows[3])
+        nc.sync.dma_start(x_planes[2][:, held:], x_rows[2][:, held:])
+        nc.sync.dma_start(wa_raw[1][:], wa_rows[:, :, N // 2 :])
 
         def turn(src, name, bank):
             turned = ps.tile([P, 4, P], F32, name=name, tag=f"bank{bank}")
@@ -170,39 +174,41 @@ def tile_list_gate_silu_kernel(
 
         x_picked = sb.tile([P, PACK, J], F32, name="x_picked")
 
-        def gather_x(i):
-            for j0, w in x_spans if i == PACK - 1 else [(0, J)]:
-                gather(x_picked[:, i, j0 : j0 + w], x_planes[i], x_list, x_wgt[:, j0 : j0 + w], j0, w)
+        def gather_x(i, j0, w):
+            gather(x_picked[:, i, j0 : j0 + w], x_planes[i], x_list, x_wgt[:, j0 : j0 + w], j0, w)
 
         last_z = len(z_spans) - 1
         for s in range(last_z):
             gate_slice(s, f"z_codes{s}")
-        gather_x(0)
+        gather_x(0, 0, J)
         gate_slice(last_z, "x_plane0")
-        for i in range(1, PACK):
-            gather_x(i)
+        gather_x(1, 0, J)
+        for j0, w in x_spans:
+            gather_x(2, j0, w)
+            gather_x(3, j0, w)
 
         wa_grouped = sb.tile([P, N, PACK], BF16, name="wa_grouped", align_bytes=64)
         wa_codes = sb.tile([P, N], U32, name="wa_codes", tag=f"x_plane{PACK - 1}", align_bytes=64)
         wa_plane = sb.tile([P, N], U8, name="wa_plane", align_bytes=64)
-        interleave(nc.scalar.copy, wa_grouped[:], wa_raw[:])
+        for h in range(2):
+            interleave(nc.scalar.copy, wa_grouped[:, h * N // 2 : (h + 1) * N // 2, :], wa_raw[h][:])
         quantize(nc, wa_codes, wa_plane, wa_grouped)
 
         out_tiles = out.rearrange("(t p) j -> p t j", p=P)
-        banks_used = 0
-        for s, (j0, w) in enumerate(x_spans):
+
+        def project(s):
+            j0, w = x_spans[s]
             grouped = sb.tile([P, w, PACK], BF16, name=f"x_grouped{s}", align_bytes=64)
             codes = sb.tile([P, w], U32, name=f"x_codes{s}", align_bytes=64)
             scales = sb.tile([P, w], U8, name=f"x_scales{s}", align_bytes=64)
-            gated = sb.tile([P, N_TILES, w], F32, name=f"gated{s}")
-            result = sb.tile([P, N_TILES, w], F32, name=f"result{s}")
-            interleave(nc.vector.tensor_copy if s == len(x_spans) - 1 else nc.scalar.copy, grouped[:], x_picked[:, :, j0 : j0 + w])
+            interleave(nc.scalar.copy, grouped[:], x_picked[:, :, j0 : j0 + w])
             quantize(nc, codes, scales, grouped)
+            sums = []
             per_bank = BANK // w
-            for t0 in range(0, N_TILES, per_bank):
-                acc = ps.tile([P, per_bank, w], F32, name=f"ya{s}_{t0}", tag=f"bank{banks_used % 8}")
-                banks_used = banks_used + 1
-                for t in range(t0, t0 + per_bank):
+            for t0, count in spans((2, 1, 1) if s == len(x_spans) - 1 else (per_bank,) * (N_TILES // per_bank)):
+                bank = (j0 * N_TILES // BANK + len(sums)) % 8
+                acc = ps.tile([P, count, w], F32, name=f"ya{s}_{t0}", tag=f"bank{bank}")
+                for t in range(t0, t0 + count):
                     nc.tensor.matmul_mx(
                         out=acc[:, t - t0, :],
                         lhsT=wa_codes[:, P * t : P * (t + 1)].bitcast(FP8X4),
@@ -212,15 +218,23 @@ def tile_list_gate_silu_kernel(
                         start=True,
                         stop=True,
                     )
+                sums.append((t0, count, acc))
+            return sums
+
+        def finish(s, sums):
+            j0, w = x_spans[s]
+            gated = sb.tile([P, N_TILES, w], F32, name=f"gated{s}")
+            result = sb.tile([P, N_TILES, w], F32, name=f"result{s}")
+            for t0, count, acc in sums:
                 nc.vector.scalar_tensor_tensor(
-                    out=gated[:, t0 : t0 + per_bank, :],
-                    in0=gate[:, t0 : t0 + per_bank, j0 : j0 + w],
+                    out=gated[:, t0 : t0 + count, :],
+                    in0=gate[:, t0 : t0 + count, j0 : j0 + w],
                     scalar=1.0,
                     in1=acc[:],
                     op0=ALU.add,
                     op1=ALU.mult,
                 )
-                for t in range(t0, t0 + per_bank):
+                for t in range(t0, t0 + count):
                     nc.scalar.activation(
                         out=result[:, t, :],
                         in_=gated[:, t, :],
@@ -228,4 +242,10 @@ def tile_list_gate_silu_kernel(
                         bias=bias[:, t : t + 1],
                         scale=0.5,
                     )
-                nc.sync.dma_start(out_tiles[:, t0 : t0 + per_bank, j0 : j0 + w], result[:, t0 : t0 + per_bank, :])
+                nc.sync.dma_start(out_tiles[:, t0 : t0 + count, j0 : j0 + w], result[:, t0 : t0 + count, :])
+
+        sums = project(0)
+        for s in range(len(x_spans)):
+            next_sums = project(s + 1) if s + 1 < len(x_spans) else None
+            finish(s, sums)
+            sums = next_sums

from contextlib import ExitStack

import concourse.mybir as mybir
from concourse.masks import make_identity

K, L, N, T, J = 512, 512, 512, 2048, 1024
FLOPS = 2 * (K + L) * N * J

F32 = mybir.dt.float32
BF16 = mybir.dt.bfloat16
I32 = mybir.dt.int32
U32 = mybir.dt.uint32
U16 = mybir.dt.uint16
U8 = mybir.dt.uint8
FP8X4 = mybir.dt.float8_e4m3fn_x4
FP4X4 = mybir.dt.float4_e2m1fn_x4
ALU = mybir.AluOpType
ACT = mybir.ActivationFunctionType

P = 128
PACK = 4
GROUP = 16
BANK = 512
N_TILES = N // P
Z_WIDTHS = (256, 256, 512)
X_WIDTHS = (256, 256, 256, 256)


def spans(widths):
    return [(sum(widths[:s]), w) for s, w in enumerate(widths)]


def interleave(copy, dst, src):
    copy(
        out=dst.rearrange("p (c e) i -> p c i e", e=4),
        in_=src.rearrange("p i (c e) -> p c i e", e=4),
    )


def quantize(nc, codes, scales, grouped):
    nc.vector.quantize_mx(
        out=codes[:].bitcast(FP8X4),
        scales=scales[:],
        in_=grouped[:].rearrange("p w i -> p (w i)"),
    )


def tile_list_gate_silu_kernel(
    tc, xT, wgt, zT, wgt2, wa, wb_words, wb_scales, b, offs, offs2, out
):
    nc = tc.nc
    with ExitStack() as ctx:
        sb = ctx.enter_context(tc.tile_pool(name="sb", bufs=1))
        ps = ctx.enter_context(tc.psum_pool(name="ps", bufs=1))

        z_spans, x_spans = spans(Z_WIDTHS), spans(X_WIDTHS)
        z_list = sb.tile([P, J // GROUP], U16, name="z_list")
        x_list = sb.tile([P, J // GROUP], U16, name="x_list")
        z_planes = [sb.tile([P, T], F32, name=f"z_plane{i}") for i in range(PACK)]
        x_planes = [sb.tile([P, T], F32, name=f"x_plane{i}", tag=f"x_plane{i}", align_bytes=64) for i in range(PACK)]
        z_wgt = sb.tile([P, J], F32, name="z_wgt")
        x_wgt = sb.tile([P, J], F32, name="x_wgt")
        wa_raw = [sb.tile([P, PACK, N // 2], F32, name=f"wa_raw{h}") for h in range(2)]
        wb_codes = sb.tile([P, 2 * N], U8, name="wb_codes", align_bytes=64)
        wb_plane = sb.tile([P, N], U8, name="wb_plane", align_bytes=64)
        bias = sb.tile([P, N_TILES], F32, name="bias")

        z_rows = zT.rearrange("(p i) t -> i p t", i=PACK)
        x_rows = xT.rearrange("(p i) t -> i p t", i=PACK)

        half_j = J // 2
        rows = sb.tile([P, half_j], F32, name="rows")
        ident = sb.tile([P, P], F32, name="ident")
        warm = sb.tile([P, 8], F32, name="warm")
        warm2 = sb.tile([P, 8], F32, name="warm2")
        nc.vector.memset(rows[:], 0.0)
        nc.vector.memset(warm[:], 0.0)
        nc.vector.memset(wb_plane[:].bitcast(I32), 0)
        nc.scalar.activation(out=warm2[:, 0:1], in_=warm[:, 0:1], func=ACT.Silu)
        make_identity(nc, ident[:])

        nc.sync.dma_start(z_list[:], offs2)
        nc.sync.dma_start(z_planes[0][:], z_rows[0])
        nc.sync.dma_start(z_wgt[:, :half_j], wgt2[:, :half_j])
        nc.sync.dma_start(z_wgt[:, half_j:], wgt2[:, half_j:])
        head_rows = wgt.rearrange("(g r) j -> r g j", r=GROUP)[0]
        nc.sync.dma_start(rows[0:8, :], head_rows[:, :half_j])
        nc.sync.dma_start(rows[8:16, :], head_rows[:, half_j:])
        nc.sync.dma_start(rows[16:20, 0:P], b.rearrange("(t p) -> t p", p=P))
        for i in range(1, PACK):
            nc.sync.dma_start(z_planes[i][:], z_rows[i])
        nc.sync.dma_start(x_list[:], offs)
        nc.sync.dma_start(x_planes[0][:], x_rows[0])
        nc.sync.dma_start(wb_codes[:].bitcast(I32), wb_words[0].bitcast(I32))
        for q in range(4):
            nc.sync.dma_start(
                wb_plane[32 * q : 32 * q + 4, :].bitcast(I32),
                wb_scales[0, 4 * q : 4 * q + 4, :].bitcast(I32),
            )
        nc.sync.dma_start(x_planes[1][:], x_rows[1])
        wa_rows = wa.rearrange("(p i) n -> p i n", i=PACK)
        held = T - T // 8
        nc.sync.dma_start(wa_raw[0][:], wa_rows[:, :, : N // 2])
        nc.sync.dma_start(x_planes[2][:, :held], x_rows[2][:, :held])
        nc.sync.dma_start(x_planes[3][:], x_rows[3])
        nc.sync.dma_start(x_planes[2][:, held:], x_rows[2][:, held:])
        nc.sync.dma_start(wa_raw[1][:], wa_rows[:, :, N // 2 :])

        def turn(src, name, bank):
            turned = ps.tile([P, 4, P], F32, name=name, tag=f"bank{bank}")
            for c in range(4):
                nc.tensor.transpose(turned[:, c, :], src[:, c * P : (c + 1) * P], ident[:])
            return turned

        def spread(turned, row0, dst, name, bank):
            wide = sb.tile([P, half_j], F32, name=name)
            nc.scalar.copy(
                out=wide[:].rearrange("p (c g r) -> p c g r", c=4, r=GROUP),
                in_=turned[:, :, row0 : row0 + 8].unsqueeze(3).to_broadcast([P, 4, 8, GROUP]),
            )
            back = turn(wide[:], name + "_back", bank)
            nc.scalar.copy(out=dst, in_=back[:].rearrange("p c j -> p (c j)"))

        turned = turn(rows[:], "turned", 0)
        spread(turned, 0, x_wgt[:, :half_j], "x_wide0", 1)
        spread(turned, 8, x_wgt[:, half_j:], "x_wide1", 2)
        nc.scalar.copy(out=bias[:], in_=turned[:, 0, 16:20])

        def gather(dst, plane, lst, weights, j0, w):
            nc.vector.tensor_tensor(
                dst,
                plane[:].indirect(lst[:, j0 // GROUP : (j0 + w) // GROUP]),
                weights,
                ALU.mult,
            )

        z_picked = sb.tile([P, PACK, J], F32, name="z_picked")
        z_grouped = [
            sb.tile([P, w, PACK], BF16, name=f"z_grouped{s}", align_bytes=64) for s, (j0, w) in enumerate(z_spans)
        ]
        for i in range(PACK):
            for j0, w in {0: spans((half_j, half_j)), PACK - 1: z_spans}.get(i, [(0, J)]):
                gather(z_picked[:, i, j0 : j0 + w], z_planes[i], z_list, z_wgt[:, j0 : j0 + w], j0, w)
            if i == 1:
                for s, (j0, w) in enumerate(z_spans):
                    interleave(nc.scalar.copy, z_grouped[s][:, :, 0:2], z_picked[:, 0:2, j0 : j0 + w])

        gate = sb.tile([P, N_TILES, J], F32, name="gate")

        def gate_slice(s, codes_tag):
            j0, w = z_spans[s]
            grouped = z_grouped[s]
            codes = sb.tile([P, w], U32, name=f"z_codes{s}", tag=codes_tag, align_bytes=64)
            scales = sb.tile([P, w], U8, name=f"z_scales{s}", align_bytes=64)
            interleave(nc.scalar.copy, grouped[:, :, 2:4], z_picked[:, 2:4, j0 : j0 + w])
            quantize(nc, codes, scales, grouped)
            per_bank = BANK // w
            for t0 in range(0, N_TILES, per_bank):
                bank = (j0 * N_TILES + t0 * w) // BANK
                acc = ps.tile([P, per_bank, w], F32, name=f"yb{s}_{t0}", tag=f"bank{bank}")
                for t in range(t0, t0 + per_bank):
                    nc.tensor.matmul_mx(
                        out=acc[:, t - t0, :],
                        lhsT=wb_codes[:, 2 * P * t : 2 * P * (t + 1)].bitcast(FP4X4),
                        lhsT_scale=wb_plane[:, P * t : P * (t + 1)],
                        rhs=codes[:].bitcast(FP8X4),
                        rhs_scale=scales[:],
                        start=True,
                        stop=True,
                    )
                nc.scalar.activation(
                    out=gate[:, t0 : t0 + per_bank, j0 : j0 + w], in_=acc[:], func=ACT.Tanh, scale=0.5
                )

        x_picked = sb.tile([P, PACK, J], F32, name="x_picked")

        def gather_x(i, j0, w):
            gather(x_picked[:, i, j0 : j0 + w], x_planes[i], x_list, x_wgt[:, j0 : j0 + w], j0, w)

        last_z = len(z_spans) - 1
        for s in range(last_z):
            gate_slice(s, f"z_codes{s}")
        gather_x(0, 0, J)
        gate_slice(last_z, "x_plane0")
        gather_x(1, 0, J)
        for j0, w in x_spans:
            gather_x(2, j0, w)
            gather_x(3, j0, w)

        wa_grouped = sb.tile([P, N, PACK], BF16, name="wa_grouped", align_bytes=64)
        wa_codes = sb.tile([P, N], U32, name="wa_codes", tag=f"x_plane{PACK - 1}", align_bytes=64)
        wa_plane = sb.tile([P, N], U8, name="wa_plane", align_bytes=64)
        for h in range(2):
            interleave(nc.scalar.copy, wa_grouped[:, h * N // 2 : (h + 1) * N // 2, :], wa_raw[h][:])
        quantize(nc, wa_codes, wa_plane, wa_grouped)

        out_tiles = out.rearrange("(t p) j -> p t j", p=P)

        def project(s):
            j0, w = x_spans[s]
            grouped = sb.tile([P, w, PACK], BF16, name=f"x_grouped{s}", align_bytes=64)
            codes = sb.tile([P, w], U32, name=f"x_codes{s}", align_bytes=64)
            scales = sb.tile([P, w], U8, name=f"x_scales{s}", align_bytes=64)
            interleave(nc.scalar.copy, grouped[:], x_picked[:, :, j0 : j0 + w])
            quantize(nc, codes, scales, grouped)
            sums = []
            per_bank = BANK // w
            for t0, count in spans((2, 1, 1) if s == len(x_spans) - 1 else (per_bank,) * (N_TILES // per_bank)):
                bank = (j0 * N_TILES // BANK + len(sums)) % 8
                acc = ps.tile([P, count, w], F32, name=f"ya{s}_{t0}", tag=f"bank{bank}")
                for t in range(t0, t0 + count):
                    nc.tensor.matmul_mx(
                        out=acc[:, t - t0, :],
                        lhsT=wa_codes[:, P * t : P * (t + 1)].bitcast(FP8X4),
                        lhsT_scale=wa_plane[:, P * t : P * (t + 1)],
                        rhs=codes[:].bitcast(FP8X4),
                        rhs_scale=scales[:],
                        start=True,
                        stop=True,
                    )
                sums.append((t0, count, acc))
            return sums

        def finish(s, sums):
            j0, w = x_spans[s]
            gated = sb.tile([P, N_TILES, w], F32, name=f"gated{s}")
            result = sb.tile([P, N_TILES, w], F32, name=f"result{s}")
            for t0, count, acc in sums:
                nc.vector.scalar_tensor_tensor(
                    out=gated[:, t0 : t0 + count, :],
                    in0=gate[:, t0 : t0 + count, j0 : j0 + w],
                    scalar=1.0,
                    in1=acc[:],
                    op0=ALU.add,
                    op1=ALU.mult,
                )
                for t in range(t0, t0 + count):
                    nc.scalar.activation(
                        out=result[:, t, :],
                        in_=gated[:, t, :],
                        func=ACT.Silu,
                        bias=bias[:, t : t + 1],
                        scale=0.5,
                    )
                nc.sync.dma_start(out_tiles[:, t0 : t0 + count, j0 : j0 + w], result[:, t0 : t0 + count, :])

        sums = project(0)
        for s in range(len(x_spans)):
            next_sums = project(s + 1) if s + 1 < len(x_spans) else None
            finish(s, sums)
            sums = next_sums
